import numpy as np
import ml_dtypes


def mxq(x, axis, fmt="e4m3"):
    dtype, down = {"e4m3": (ml_dtypes.float8_e4m3fn, 7), "e5m2": (ml_dtypes.float8_e5m2, 14)}[fmt]
    v = np.moveaxis(np.asarray(x, np.float32).astype(ml_dtypes.bfloat16).astype(np.float64), axis, -1)
    blocks = v.reshape(v.shape[:-1] + (-1, 32))
    amax = np.abs(blocks).max(-1, keepdims=True)
    byte = np.maximum(np.where(amax > 0, np.frexp(amax)[1] - 1 + 127, 0) - down, 1)
    scale = np.exp2(byte - 127.0)
    codes = (blocks / scale).astype(np.float32).astype(dtype).astype(np.float64)
    return np.moveaxis((codes * scale).reshape(v.shape), -1, axis)


WIDE = False


def mx_kscale(k):
    if not WIDE:
        return np.ones(k)
    levels = np.array([10, -10, 5, -5, 0])
    if k % 512:
        return np.exp2(np.random.permutation(np.resize(levels, k // 32))).repeat(32)
    a = np.empty((k // 512, 16))
    for p in range(k // 512):
        a[p, :8] = np.random.permutation(np.resize(levels, 8))
        for g in range(8):
            far = levels[np.abs(levels - a[p, g]) >= 10]
            a[p, g + 8] = far[np.random.randint(len(far))]
    return np.exp2(a.ravel()).repeat(32)


def f64(x):
    return np.asarray(x).astype(np.float64)


def striped(idx):
    return np.tile(idx.reshape(-1, 16).T, (8, 1)).astype(np.uint16)


def unstriped(offs):
    return offs[:16].T.reshape(-1).astype(np.int64)


E2M1 = np.array([0.0, 0.5, 1.0, 1.5, 2.0, 3.0, 4.0, 6.0, -0.0, -0.5, -1.0, -1.5, -2.0, -3.0, -4.0, -6.0])


def pack_weight(w, fmt):
    k, n = w.shape
    w = f64(np.asarray(w, np.float32).astype(ml_dtypes.bfloat16)).reshape(k // 32, 32, n)
    amax = np.abs(w).max(1)
    if fmt == "e4m3":
        byte = np.frexp(amax)[1] - 1 + 127 - 7
    else:
        mant, ex = np.frexp(amax / 6.0)
        byte = np.where(mant > 0.5, ex, ex - 1) + 127
    byte = np.clip(np.where(amax > 0, byte, 1), 1, 254)
    scaled = (w * np.exp2(127.0 - byte)[:, None, :]).reshape(k, n).astype(np.float32)
    by_word = np.ascontiguousarray(scaled.reshape(k // 512, 128, 4, n).transpose(0, 1, 3, 2))
    if fmt == "e4m3":
        words = by_word.astype(ml_dtypes.float8_e4m3fn).view(np.uint8)
    else:
        c = by_word.astype(ml_dtypes.float4_e2m1fn).view(np.uint8) & 0xF
        words = (c[..., 0::2] | (c[..., 1::2] << 4)).reshape(k // 512, 128, 2 * n)
    return np.ascontiguousarray(words), np.ascontiguousarray(byte.astype(np.uint8).reshape(k // 512, 16, n))


def unpack_weight(words, scales, fmt):
    g, _, n = scales.shape
    words = np.ascontiguousarray(words).reshape(g, 128, n, -1)
    if fmt == "e4m3":
        vals = words.view(ml_dtypes.float8_e4m3fn).astype(np.float64)
    else:
        nib = np.empty((g, 128, n, 4), np.uint8)
        nib[..., 0::2] = words & 0xF
        nib[..., 1::2] = words >> 4
        vals = E2M1[nib]
    vals = vals * np.repeat(np.exp2(scales.astype(np.float64) - 127.0), 8, axis=1)[..., None]
    return vals.transpose(0, 1, 3, 2).reshape(g * 512, n)


K, T, E, C, N = 512, 384, 6, 128, 256


def by_expert(wq, xq):
    return np.concatenate([wq[e].T @ xq[:, e * C:(e + 1) * C] for e in range(E)], axis=1)


def setup_inputs():
    n = np.random.standard_normal
    s = mx_kscale(K)[:, None]
    first = np.random.permutation(np.repeat(np.arange(E), T // E))
    second = (first + 1 + np.random.permutation(np.repeat(np.arange(E - 1), -(-T // (E - 1)))[:T])) % E
    while np.bincount(second, minlength=E).max() != T // E:
        load = np.bincount(second, minlength=E); hi, lo = int(load.argmax()), int(load.argmin())
        t = np.flatnonzero((second == hi) & (first != lo))[0]; second[t] = lo
    slot_token = np.empty(E * C, np.int64); pos = np.empty((2, T), np.int64); fill = np.zeros(E, np.int64)
    place = np.stack([np.random.permutation(C) for _ in range(E)])
    for r, deal in enumerate((first, second)):
        for t in np.random.permutation(T):
            e = deal[t]; j = e * C + place[e, fill[e]]; fill[e] += 1; slot_token[j] = t; pos[r, t] = j
    g = np.random.uniform(0.2, 0.8, T)
    w = [pack_weight(m, "e2m1") for m in n((E + 1, K, N)) / np.sqrt(K) / s[None]]
    return {
        "xT": (n((K, T)) * s).astype(np.float32),
        "w_words": np.stack([m[0] for m in w]),
        "w_scales": np.stack([m[1] for m in w]),
        "b": (0.3 * n((N, E + 1))).astype(np.float32),
        "gate": np.stack([np.tile(g, (N, 1)), np.tile(1.0 - g, (N, 1))]).astype(np.float32),
        "offs": striped(slot_token),
        "pos1": striped(pos[0]),
        "pos2": striped(pos[1]),
    }


def reference(xT, w_words, w_scales, b, gate, offs, pos1, pos2):
    idx = unstriped(offs)
    w = np.stack([unpack_weight(w_words[e], w_scales[e], "e2m1") for e in range(E + 1)])
    wq = w
    xs = mxq(f64(xT), 0, "e4m3")
    ys = (wq[E].T @ xs) + f64(b)[:, E:]
    xq = mxq(f64(xT)[:, idx], 0, "e4m3")
    y = by_expert(w, xq)
    y = y + np.repeat(f64(b)[:, :E], C, axis=1)
    return ys + f64(gate[0]) * y[:, unstriped(pos1)] + f64(gate[1]) * y[:, unstriped(pos2)]

@@ -1,0 +1,182 @@
+from contextlib import ExitStack
+
+import concourse.mybir as mybir
+
+K, T, E, C, N = 512, 384, 6, 128, 256
+S = E * C
+P = 128
+HALVES = N // P
+FLOPS = 2 * K * N * (S + T)
+
+F32 = mybir.dt.float32
+BF16 = mybir.dt.bfloat16
+I32 = mybir.dt.int32
+U32 = mybir.dt.uint32
+U16 = mybir.dt.uint16
+U8 = mybir.dt.uint8
+E4M3X4 = mybir.dt.float8_e4m3fn_x4
+E2M1X4 = mybir.dt.float4_e2m1fn_x4
+
+ADD, MULT = mybir.AluOpType.add, mybir.AluOpType.mult
+COPY, IDENTITY = mybir.ActivationFunctionType.Copy, mybir.ActivationFunctionType.Identity
+
+WINDOW = 1024
+
+
+def tile_moe_shr_lin_bias_kernel(tc, xT, w_words, w_scales, b, gate, offs, pos1, pos2, out):
+    nc = tc.nc
+    with ExitStack() as ctx:
+        lists = ctx.enter_context(tc.tile_pool(name="lists", bufs=1))
+        keep = ctx.enter_context(tc.tile_pool(name="keep", bufs=1))
+        psum = ctx.enter_context(tc.psum_pool(name="psum", bufs=1))
+
+        offs_sb = lists.tile([P, S // 16], U16, name="offs_sb")
+        pos1_sb = lists.tile([P, T // 16], U16, name="pos1_sb")
+        pos2_sb = lists.tile([P, T // 16], U16, name="pos2_sb")
+
+        x_raw = [keep.tile([P, 2, T], F32, name=f"x_raw{u}") for u in range(2)]
+        pairs = [keep.tile([P, WINDOW], U32, name=f"pairs{u}") for u in range(2)]
+        slot_x = keep.tile([P, 2 * S], U32, name="slot_x", align_bytes=64)
+        token_x = keep.tile([P, 4 * T], BF16, name="token_x", align_bytes=64)
+        slot_codes = keep.tile([P, S], U32, name="slot_codes", align_bytes=64)
+        slot_scales = keep.tile([P, S], U8, name="slot_scales", align_bytes=64)
+        token_codes = keep.tile([P, T], U32, name="token_codes", align_bytes=64)
+        token_scales = keep.tile([P, T], U8, name="token_scales", align_bytes=64)
+        words = keep.tile([P, E + 1, 2 * N], U8, name="words", align_bytes=64)
+        scales = keep.tile([P, E + 1, N], U8, name="scales", align_bytes=64)
+        bias = keep.tile([P, HALVES, E + 1], F32, name="bias")
+        gates = keep.tile([P, 2, HALVES, T], F32, name="gates")
+        y = [keep.tile([P, S], F32, name=f"y{h}") for h in range(HALVES)]
+        first = [keep.tile([P, T], F32, name=f"first{h}") for h in range(HALVES)]
+        second = [keep.tile([P, T], F32, name=f"second{h}") for h in range(HALVES)]
+        partial = [keep.tile([P, T], F32, name=f"partial{h}") for h in range(HALVES)]
+        result = [keep.tile([P, T], F32, name=f"result{h}") for h in range(HALVES)]
+        warm = keep.tile([P, 2], F32, name="warm")
+        y_ps = [[psum.tile([P, 2 * C], F32, name=f"y_ps{g}_{h}") for h in range(HALVES)] for g in range(E // 2)]
+        ys_ps = [psum.tile([P, T], F32, name=f"ys_ps{h}") for h in range(HALVES)]
+
+        x_view = xT.rearrange("(p u i) t -> p u i t", u=2, i=2)
+        nc.sync.dma_start(out=x_raw[0][:], in_=x_view[:, 0])
+        nc.sync.dma_start(offs_sb[:], offs)
+        nc.sync.dma_start(out=x_raw[1][:], in_=x_view[:, 1])
+
+        nc.vector.memset(scales[:].rearrange("p e n -> p (e n)").bitcast(I32), 0)
+        nc.vector.memset(warm[:, 0:1], 0.0)
+        nc.scalar.activation(warm[:, 1:2], warm[:, 0:1], IDENTITY)
+        for u in range(2):
+            nc.gpsimd.memset(pairs[u][:, T:], 0)
+
+        w_scales_i = w_scales.bitcast(I32)
+        for q in range(4):
+            nc.sync.dma_start(
+                out=scales[32 * q : 32 * q + 4].bitcast(I32),
+                in_=w_scales_i[:, 0, 4 * q : 4 * q + 4, :].rearrange("e q n -> q e n"),
+            )
+        nc.sync.dma_start(out=words[:].bitcast(I32), in_=w_words.bitcast(I32).rearrange("e a p x -> p (e a) x"))
+        nc.sync.dma_start(out=bias[:], in_=b.rearrange("(h p) e -> p h e", p=P))
+        nc.sync.dma_start(pos1_sb[:], pos1)
+        nc.sync.dma_start(pos2_sb[:], pos2)
+        nc.sync.dma_start(out=gates[:], in_=gate.rearrange("g (h p) t -> p g h t", p=P))
+
+        def round_pairs(engine_copy, u):
+            engine_copy(
+                pairs[u][:, 0:T].bitcast(BF16).rearrange("p (t i) -> p t i", i=2),
+                x_raw[u][:].rearrange("p i t -> p t i"),
+            )
+
+        slot_pairs = slot_x[:].rearrange("p (s u) -> p s u", u=2)
+
+        def gather(u, lo, hi):
+            nc.vector.tensor_copy(
+                slot_pairs[:, lo:hi, u],
+                pairs[u][:].indirect(offs_sb[:, lo // 16 : hi // 16]),
+            )
+
+        def quantize_slots(lo, hi):
+            nc.vector.quantize_mx(
+                out=slot_codes[:, lo:hi].bitcast(E4M3X4),
+                scales=slot_scales[:, lo:hi],
+                in_=slot_x[:, 2 * lo : 2 * hi].bitcast(BF16),
+            )
+
+        def quantize_tokens(lo, hi):
+            nc.vector.quantize_mx(
+                out=token_codes[:, lo:hi].bitcast(E4M3X4),
+                scales=token_scales[:, lo:hi],
+                in_=token_x[:, 4 * lo : 4 * hi],
+            )
+
+        def multiply(acc, e, h, codes, code_scales):
+            nc.tensor.matmul_mx(
+                out=acc,
+                lhsT=words[:, e, 2 * P * h : 2 * P * (h + 1)].bitcast(E2M1X4),
+                lhsT_scale=scales[:, e, P * h : P * (h + 1)],
+                rhs=codes.bitcast(E4M3X4),
+                rhs_scale=code_scales,
+                start=True,
+                stop=True,
+            )
+
+        def expert(e):
+            lo, hi = e * C, (e + 1) * C
+            cols = slice((e % 2) * C, (e % 2 + 1) * C)
+            for h in range(HALVES):
+                multiply(y_ps[e // 2][h][:, cols], e, h, slot_codes[:, lo:hi], slot_scales[:, lo:hi])
+            for h in range(HALVES):
+                nc.scalar.activation(y[h][:, lo:hi], y_ps[e // 2][h][:, cols], IDENTITY, bias=bias[:, h, e : e + 1])
+
+        def shared(lo, hi):
+            for h in range(HALVES):
+                multiply(ys_ps[h][:, lo:hi], E, h, token_codes[:, lo:hi], token_scales[:, lo:hi])
+
+        round_pairs(nc.vector.tensor_copy, 0)
+        round_pairs(nc.scalar.copy, 1)
+        token_view = token_x[:].rearrange("p (t u i) -> p t u i", u=2, i=2)
+        for u in range(2):
+            nc.scalar.copy(token_view[:, :, u, :], x_raw[u][:].rearrange("p i t -> p t i"))
+
+        gather(0, 0, S)
+        gather(1, 0, 256)
+        gather(1, 256, 512)
+        quantize_slots(0, 256)
+        expert(0)
+        expert(1)
+        gather(1, 512, 640)
+        quantize_slots(256, 512)
+        expert(2)
+        expert(3)
+        gather(1, 640, 768)
+        quantize_slots(512, 640)
+        expert(4)
+        quantize_tokens(256, 384)
+        quantize_slots(640, 768)
+        expert(5)
+        quantize_tokens(0, 256)
+        shared(256, 384)
+        shared(0, 256)
+
+        def fetch(dst, h, g, lo, hi):
+            nc.vector.tensor_tensor(
+                dst[:, lo:hi],
+                y[h][:].indirect((pos1_sb, pos2_sb)[g][:, lo // 16 : hi // 16]),
+                gates[:, g, h, lo:hi],
+                MULT,
+            )
+
+        def add_shared(h):
+            nc.vector.scalar_tensor_tensor(partial[h][:], ys_ps[h][:], bias[:, h, E : E + 1], first[h][:], ADD, ADD)
+
+        def finish(h, lo, hi):
+            nc.vector.tensor_tensor(result[h][:, lo:hi], partial[h][:, lo:hi], second[h][:, lo:hi], ADD)
+            nc.sync.dma_start(out=out[h * P : (h + 1) * P, lo:hi], in_=result[h][:, lo:hi])
+
+        fetch(first[0], 0, 0, 0, T)
+        fetch(second[0], 0, 1, 0, T)
+        add_shared(0)
+        fetch(first[1], 1, 0, 0, T)
+        finish(0, 0, T)
+        add_shared(1)
+        fetch(second[1], 1, 1, 0, 192)
+        fetch(second[1], 1, 1, 192, T)
+        finish(1, 0, 192)
+        finish(1, 192, T)

@@ -36,7 +36,8 @@ def tile_moe_shr_lin_bias_kernel(tc, xT, w_words, w_scales, b, gate, offs, pos1,
 
         x_raw = [keep.tile([P, 2, T], F32, name=f"x_raw{u}") for u in range(2)]
         pairs = [keep.tile([P, WINDOW], U32, name=f"pairs{u}") for u in range(2)]
-        slot_x = keep.tile([P, 2 * S], U32, name="slot_x", align_bytes=64)
+        slot_x = keep.tile([P, 2 * S], I32, name="slot_x", align_bytes=64)
+        picked = keep.tile([P, 2, S], U32, name="picked")
         token_x = keep.tile([P, 4 * T], BF16, name="token_x", align_bytes=64)
         slot_codes = keep.tile([P, S], U32, name="slot_codes", align_bytes=64)
         slot_scales = keep.tile([P, S], U8, name="slot_scales", align_bytes=64)
@@ -56,7 +57,8 @@ def tile_moe_shr_lin_bias_kernel(tc, xT, w_words, w_scales, b, gate, offs, pos1,
         ys_ps = [psum.tile([P, T], F32, name=f"ys_ps{h}") for h in range(HALVES)]
 
         x_view = xT.rearrange("(p u i) t -> p u i t", u=2, i=2)
-        nc.sync.dma_start(out=x_raw[0][:], in_=x_view[:, 0])
+        nc.sync.dma_start(out=x_raw[0][:, :, 0:256], in_=x_view[:, 0, :, 0:256])
+        nc.sync.dma_start(out=x_raw[0][:, :, 256:T], in_=x_view[:, 0, :, 256:T])
         nc.sync.dma_start(offs_sb[:], offs)
         nc.sync.dma_start(out=x_raw[1][:], in_=x_view[:, 1])
 
@@ -78,18 +80,19 @@ def tile_moe_shr_lin_bias_kernel(tc, xT, w_words, w_scales, b, gate, offs, pos1,
         nc.sync.dma_start(pos2_sb[:], pos2)
         nc.sync.dma_start(out=gates[:], in_=gate.rearrange("g (h p) t -> p g h t", p=P))
 
-        def round_pairs(engine_copy, u):
+        def round_pairs(engine_copy, u, lo, hi):
             engine_copy(
-                pairs[u][:, 0:T].bitcast(BF16).rearrange("p (t i) -> p t i", i=2),
-                x_raw[u][:].rearrange("p i t -> p t i"),
+                pairs[u][:, lo:hi].bitcast(BF16).rearrange("p (t i) -> p t i", i=2),
+                x_raw[u][:, :, lo:hi].rearrange("p i t -> p t i"),
             )
 
-        slot_pairs = slot_x[:].rearrange("p (s u) -> p s u", u=2)
-
         def gather(u, lo, hi):
+            nc.vector.tensor_copy(picked[:, u, lo:hi], pairs[u][:].indirect(offs_sb[:, lo // 16 : hi // 16]))
+
+        def interleave(lo, hi):
             nc.vector.tensor_copy(
-                slot_pairs[:, lo:hi, u],
-                pairs[u][:].indirect(offs_sb[:, lo // 16 : hi // 16]),
+                slot_x[:, 2 * lo : 2 * hi].rearrange("p (s u) -> p s u", u=2),
+                picked[:, :, lo:hi].bitcast(I32).rearrange("p u s -> p s u"),
             )
 
         def quantize_slots(lo, hi):
@@ -129,8 +132,9 @@ def tile_moe_shr_lin_bias_kernel(tc, xT, w_words, w_scales, b, gate, offs, pos1,
             for h in range(HALVES):
                 multiply(ys_ps[h][:, lo:hi], E, h, token_codes[:, lo:hi], token_scales[:, lo:hi])
 
-        round_pairs(nc.vector.tensor_copy, 0)
-        round_pairs(nc.scalar.copy, 1)
+        round_pairs(nc.vector.tensor_copy, 0, 0, 256)
+        round_pairs(nc.vector.tensor_copy, 0, 256, T)
+        round_pairs(nc.scalar.copy, 1, 0, T)
         token_view = token_x[:].rearrange("p (t u i) -> p t u i", u=2, i=2)
         for u in range(2):
             nc.scalar.copy(token_view[:, :, u, :], x_raw[u][:].rearrange("p i t -> p t i"))
@@ -138,20 +142,24 @@ def tile_moe_shr_lin_bias_kernel(tc, xT, w_words, w_scales, b, gate, offs, pos1,
         gather(0, 0, S)
         gather(1, 0, 256)
         gather(1, 256, 512)
+        interleave(0, 256)
+        gather(1, 512, 640)
         quantize_slots(0, 256)
         expert(0)
         expert(1)
-        gather(1, 512, 640)
+        interleave(256, 512)
+        gather(1, 640, 768)
         quantize_slots(256, 512)
         expert(2)
         expert(3)
-        gather(1, 640, 768)
+        interleave(512, 640)
+        quantize_tokens(256, 384)
         quantize_slots(512, 640)
         expert(4)
-        quantize_tokens(256, 384)
+        interleave(640, 768)
+        quantize_tokens(0, 256)
         quantize_slots(640, 768)
         expert(5)
-        quantize_tokens(0, 256)
         shared(256, 384)
         shared(0, 256)
 

@@ -34,8 +34,8 @@ def tile_moe_shr_lin_bias_kernel(tc, xT, w_words, w_scales, b, gate, offs, pos1,
         pos1_sb = lists.tile([P, T // 16], U16, name="pos1_sb")
         pos2_sb = lists.tile([P, T // 16], U16, name="pos2_sb")
 
-        x_raw = [keep.tile([P, 2, T], F32, name=f"x_raw{u}") for u in range(2)]
-        pairs = [keep.tile([P, WINDOW], U32, name=f"pairs{u}") for u in range(2)]
+        x_raw = keep.tile([P, 2, 2, T], F32, name="x_raw")
+        pairs = keep.tile([P, 2, WINDOW], U32, name="pairs")
         slot_x = keep.tile([P, 2 * S], I32, name="slot_x", align_bytes=64)
         picked = keep.tile([P, 2, S], U32, name="picked")
         token_x = keep.tile([P, 4 * T], BF16, name="token_x", align_bytes=64)
@@ -57,16 +57,16 @@ def tile_moe_shr_lin_bias_kernel(tc, xT, w_words, w_scales, b, gate, offs, pos1,
         ys_ps = [psum.tile([P, T], F32, name=f"ys_ps{h}") for h in range(HALVES)]
 
         x_view = xT.rearrange("(p u i) t -> p u i t", u=2, i=2)
-        nc.sync.dma_start(out=x_raw[0][:, :, 0:256], in_=x_view[:, 0, :, 0:256])
-        nc.sync.dma_start(out=x_raw[0][:, :, 256:T], in_=x_view[:, 0, :, 256:T])
+        nc.sync.dma_start(out=x_raw[:, 0, :, 0:256], in_=x_view[:, 0, :, 0:256])
+        nc.sync.dma_start(out=x_raw[:, 0, :, 256:T], in_=x_view[:, 0, :, 256:T])
         nc.sync.dma_start(offs_sb[:], offs)
-        nc.sync.dma_start(out=x_raw[1][:], in_=x_view[:, 1])
+        nc.sync.dma_start(out=x_raw[:, 1], in_=x_view[:, 1])
 
         nc.vector.memset(scales[:].rearrange("p e n -> p (e n)").bitcast(I32), 0)
         nc.vector.memset(warm[:, 0:1], 0.0)
         nc.scalar.activation(warm[:, 1:2], warm[:, 0:1], IDENTITY)
         for u in range(2):
-            nc.gpsimd.memset(pairs[u][:, T:], 0)
+            nc.gpsimd.memset(pairs[:, u, T:], 0)
 
         w_scales_i = w_scales.bitcast(I32)
         for q in range(4):
@@ -82,17 +82,23 @@ def tile_moe_shr_lin_bias_kernel(tc, xT, w_words, w_scales, b, gate, offs, pos1,
 
         def round_pairs(engine_copy, u, lo, hi):
             engine_copy(
-                pairs[u][:, lo:hi].bitcast(BF16).rearrange("p (t i) -> p t i", i=2),
-                x_raw[u][:, :, lo:hi].rearrange("p i t -> p t i"),
+                pairs[:, u, lo:hi].bitcast(BF16).rearrange("p (t i) -> p t i", i=2),
+                x_raw[:, u, :, lo:hi].rearrange("p i t -> p t i"),
             )
 
         def gather(u, lo, hi):
-            nc.vector.tensor_copy(picked[:, u, lo:hi], pairs[u][:].indirect(offs_sb[:, lo // 16 : hi // 16]))
+            nc.vector.tensor_copy(picked[:, u, lo:hi], pairs[:, u, :].indirect(offs_sb[:, lo // 16 : hi // 16]))
 
         def interleave(lo, hi):
             nc.vector.tensor_copy(
                 slot_x[:, 2 * lo : 2 * hi].rearrange("p (s u) -> p s u", u=2),
                 picked[:, :, lo:hi].bitcast(I32).rearrange("p u s -> p s u"),
+            )
+
+        def interleave_on_scalar(lo, hi):
+            nc.scalar.copy(
+                slot_x[:, 2 * lo : 2 * hi].bitcast(BF16).rearrange("p (s u i) -> p s u i", u=2, i=2),
+                picked[:, :, lo:hi].bitcast(BF16).rearrange("p u (s i) -> p s u i", i=2),
             )
 
         def quantize_slots(lo, hi):
@@ -120,13 +126,22 @@ def tile_moe_shr_lin_bias_kernel(tc, xT, w_words, w_scales, b, gate, offs, pos1,
                 stop=True,
             )
 
-        def expert(e):
+        def products(experts):
+            for h in range(HALVES):
+                for e in experts:
+                    product(e, h)
+
+        def product(e, h):
             lo, hi = e * C, (e + 1) * C
-            cols = slice((e % 2) * C, (e % 2 + 1) * C)
-            for h in range(HALVES):
-                multiply(y_ps[e // 2][h][:, cols], e, h, slot_codes[:, lo:hi], slot_scales[:, lo:hi])
-            for h in range(HALVES):
-                nc.scalar.activation(y[h][:, lo:hi], y_ps[e // 2][h][:, cols], IDENTITY, bias=bias[:, h, e : e + 1])
+            multiply(y_ps[e // 2][h][:, (e % 2) * C : (e % 2 + 1) * C], e, h, slot_codes[:, lo:hi], slot_scales[:, lo:hi])
+
+        def empty(e, h):
+            nc.scalar.activation(
+                y[h][:, e * C : (e + 1) * C],
+                y_ps[e // 2][h][:, (e % 2) * C : (e % 2 + 1) * C],
+                IDENTITY,
+                bias=bias[:, h, e : e + 1],
+            )
 
         def shared(lo, hi):
             for h in range(HALVES):
@@ -135,31 +150,35 @@ def tile_moe_shr_lin_bias_kernel(tc, xT, w_words, w_scales, b, gate, offs, pos1,
         round_pairs(nc.vector.tensor_copy, 0, 0, 256)
         round_pairs(nc.vector.tensor_copy, 0, 256, T)
         round_pairs(nc.scalar.copy, 1, 0, T)
-        token_view = token_x[:].rearrange("p (t u i) -> p t u i", u=2, i=2)
-        for u in range(2):
-            nc.scalar.copy(token_view[:, :, u, :], x_raw[u][:].rearrange("p i t -> p t i"))
+        nc.scalar.copy(
+            token_x[:].rearrange("p (t u i) -> p t u i", u=2, i=2),
+            pairs[:, :, 0:T].bitcast(BF16).rearrange("p u (t i) -> p t u i", i=2),
+        )
 
         gather(0, 0, S)
         gather(1, 0, 256)
         gather(1, 256, 512)
+        interleave_on_scalar(256, 512)
         interleave(0, 256)
-        gather(1, 512, 640)
+        gather(1, 512, 768)
         quantize_slots(0, 256)
-        expert(0)
-        expert(1)
-        interleave(256, 512)
-        gather(1, 640, 768)
+        products((0, 1))
+        for h in range(HALVES):
+            for e in (0, 1):
+                empty(e, h)
+        interleave(512, 768)
         quantize_slots(256, 512)
-        expert(2)
-        expert(3)
-        interleave(512, 640)
+        products((2, 3))
+        empty(2, 0)
+        empty(3, 0)
+        quantize_slots(512, 768)
+        products((4, 5))
+        empty(4, 0)
+        empty(5, 0)
+        for e in range(2, E):
+            empty(e, 1)
         quantize_tokens(256, 384)
-        quantize_slots(512, 640)
-        expert(4)
-        interleave(640, 768)
         quantize_tokens(0, 256)
-        quantize_slots(640, 768)
-        expert(5)
         shared(256, 384)
         shared(0, 256)
 
@@ -183,8 +202,8 @@ def tile_moe_shr_lin_bias_kernel(tc, xT, w_words, w_scales, b, gate, offs, pos1,
         add_shared(0)
         fetch(first[1], 1, 0, 0, T)
         finish(0, 0, T)
+        fetch(second[1], 1, 1, 0, 256)
         add_shared(1)
-        fetch(second[1], 1, 1, 0, 192)
-        fetch(second[1], 1, 1, 192, T)
-        finish(1, 0, 192)
-        finish(1, 192, T)
+        fetch(second[1], 1, 1, 256, T)
+        finish(1, 0, 256)
+        finish(1, 256, T)

from contextlib import ExitStack

import concourse.mybir as mybir

K, T, E, C, N = 512, 384, 6, 128, 256
S = E * C
P = 128
HALVES = N // P
FLOPS = 2 * K * N * (S + T)

F32 = mybir.dt.float32
BF16 = mybir.dt.bfloat16
I32 = mybir.dt.int32
U32 = mybir.dt.uint32
U16 = mybir.dt.uint16
U8 = mybir.dt.uint8
E4M3X4 = mybir.dt.float8_e4m3fn_x4
E2M1X4 = mybir.dt.float4_e2m1fn_x4

ADD, MULT = mybir.AluOpType.add, mybir.AluOpType.mult
COPY, IDENTITY = mybir.ActivationFunctionType.Copy, mybir.ActivationFunctionType.Identity

WINDOW = 1024


def tile_moe_shr_lin_bias_kernel(tc, xT, w_words, w_scales, b, gate, offs, pos1, pos2, out):
    nc = tc.nc
    with ExitStack() as ctx:
        lists = ctx.enter_context(tc.tile_pool(name="lists", bufs=1))
        keep = ctx.enter_context(tc.tile_pool(name="keep", bufs=1))
        psum = ctx.enter_context(tc.psum_pool(name="psum", bufs=1))

        offs_sb = lists.tile([P, S // 16], U16, name="offs_sb")
        pos1_sb = lists.tile([P, T // 16], U16, name="pos1_sb")
        pos2_sb = lists.tile([P, T // 16], U16, name="pos2_sb")

        x_raw = keep.tile([P, 2, 2, T], F32, name="x_raw")
        pairs = keep.tile([P, 2, WINDOW], U32, name="pairs")
        slot_x = keep.tile([P, 2 * S], I32, name="slot_x", align_bytes=64)
        picked = keep.tile([P, 2, S], U32, name="picked")
        token_x = keep.tile([P, 4 * T], BF16, name="token_x", align_bytes=64)
        slot_codes = keep.tile([P, S], U32, name="slot_codes", align_bytes=64)
        slot_scales = keep.tile([P, S], U8, name="slot_scales", align_bytes=64)
        token_codes = keep.tile([P, T], U32, name="token_codes", align_bytes=64)
        token_scales = keep.tile([P, T], U8, name="token_scales", align_bytes=64)
        words = keep.tile([P, E + 1, 2 * N], U8, name="words", align_bytes=64)
        scales = keep.tile([P, E + 1, N], U8, name="scales", align_bytes=64)
        bias = keep.tile([P, HALVES, E + 1], F32, name="bias")
        gates = keep.tile([P, 2, HALVES, T], F32, name="gates")
        y = [keep.tile([P, S], F32, name=f"y{h}") for h in range(HALVES)]
        first = [keep.tile([P, T], F32, name=f"first{h}") for h in range(HALVES)]
        second = [keep.tile([P, T], F32, name=f"second{h}") for h in range(HALVES)]
        partial = [keep.tile([P, T], F32, name=f"partial{h}") for h in range(HALVES)]
        result = [keep.tile([P, T], F32, name=f"result{h}") for h in range(HALVES)]
        warm = keep.tile([P, 2], F32, name="warm")
        y_ps = [[psum.tile([P, 2 * C], F32, name=f"y_ps{g}_{h}") for h in range(HALVES)] for g in range(E // 2)]
        ys_ps = [psum.tile([P, T], F32, name=f"ys_ps{h}") for h in range(HALVES)]

        x_view = xT.rearrange("(p u i) t -> p u i t", u=2, i=2)
        nc.sync.dma_start(out=x_raw[:, 0, :, 0:256], in_=x_view[:, 0, :, 0:256])
        nc.sync.dma_start(out=x_raw[:, 0, :, 256:T], in_=x_view[:, 0, :, 256:T])
        nc.sync.dma_start(offs_sb[:], offs)
        nc.sync.dma_start(out=x_raw[:, 1], in_=x_view[:, 1])

        nc.vector.memset(scales[:].rearrange("p e n -> p (e n)").bitcast(I32), 0)
        nc.vector.memset(warm[:, 0:1], 0.0)
        nc.scalar.activation(warm[:, 1:2], warm[:, 0:1], IDENTITY)
        for u in range(2):
            nc.gpsimd.memset(pairs[:, u, T:], 0)

        w_scales_i = w_scales.bitcast(I32)
        for q in range(4):
            nc.sync.dma_start(
                out=scales[32 * q : 32 * q + 4].bitcast(I32),
                in_=w_scales_i[:, 0, 4 * q : 4 * q + 4, :].rearrange("e q n -> q e n"),
            )
        nc.sync.dma_start(out=words[:].bitcast(I32), in_=w_words.bitcast(I32).rearrange("e a p x -> p (e a) x"))
        nc.sync.dma_start(out=bias[:], in_=b.rearrange("(h p) e -> p h e", p=P))
        nc.sync.dma_start(pos1_sb[:], pos1)
        nc.sync.dma_start(pos2_sb[:], pos2)
        nc.sync.dma_start(out=gates[:], in_=gate.rearrange("g (h p) t -> p g h t", p=P))

        def round_pairs(engine_copy, u, lo, hi):
            engine_copy(
                pairs[:, u, lo:hi].bitcast(BF16).rearrange("p (t i) -> p t i", i=2),
                x_raw[:, u, :, lo:hi].rearrange("p i t -> p t i"),
            )

        def gather(u, lo, hi):
            nc.vector.tensor_copy(picked[:, u, lo:hi], pairs[:, u, :].indirect(offs_sb[:, lo // 16 : hi // 16]))

        def interleave(lo, hi):
            nc.vector.tensor_copy(
                slot_x[:, 2 * lo : 2 * hi].rearrange("p (s u) -> p s u", u=2),
                picked[:, :, lo:hi].bitcast(I32).rearrange("p u s -> p s u"),
            )

        def interleave_on_scalar(lo, hi):
            nc.scalar.copy(
                slot_x[:, 2 * lo : 2 * hi].bitcast(BF16).rearrange("p (s u i) -> p s u i", u=2, i=2),
                picked[:, :, lo:hi].bitcast(BF16).rearrange("p u (s i) -> p s u i", i=2),
            )

        def quantize_slots(lo, hi):
            nc.vector.quantize_mx(
                out=slot_codes[:, lo:hi].bitcast(E4M3X4),
                scales=slot_scales[:, lo:hi],
                in_=slot_x[:, 2 * lo : 2 * hi].bitcast(BF16),
            )

        def quantize_tokens(lo, hi):
            nc.vector.quantize_mx(
                out=token_codes[:, lo:hi].bitcast(E4M3X4),
                scales=token_scales[:, lo:hi],
                in_=token_x[:, 4 * lo : 4 * hi],
            )

        def multiply(acc, e, h, codes, code_scales):
            nc.tensor.matmul_mx(
                out=acc,
                lhsT=words[:, e, 2 * P * h : 2 * P * (h + 1)].bitcast(E2M1X4),
                lhsT_scale=scales[:, e, P * h : P * (h + 1)],
                rhs=codes.bitcast(E4M3X4),
                rhs_scale=code_scales,
                start=True,
                stop=True,
            )

        def products(experts):
            for h in range(HALVES):
                for e in experts:
                    product(e, h)

        def product(e, h):
            lo, hi = e * C, (e + 1) * C
            multiply(y_ps[e // 2][h][:, (e % 2) * C : (e % 2 + 1) * C], e, h, slot_codes[:, lo:hi], slot_scales[:, lo:hi])

        def empty(e, h):
            nc.scalar.activation(
                y[h][:, e * C : (e + 1) * C],
                y_ps[e // 2][h][:, (e % 2) * C : (e % 2 + 1) * C],
                IDENTITY,
                bias=bias[:, h, e : e + 1],
            )

        def shared(lo, hi):
            for h in range(HALVES):
                multiply(ys_ps[h][:, lo:hi], E, h, token_codes[:, lo:hi], token_scales[:, lo:hi])

        round_pairs(nc.vector.tensor_copy, 0, 0, 256)
        round_pairs(nc.vector.tensor_copy, 0, 256, T)
        round_pairs(nc.scalar.copy, 1, 0, T)
        nc.scalar.copy(
            token_x[:].rearrange("p (t u i) -> p t u i", u=2, i=2),
            pairs[:, :, 0:T].bitcast(BF16).rearrange("p u (t i) -> p t u i", i=2),
        )

        gather(0, 0, S)
        gather(1, 0, 256)
        gather(1, 256, 512)
        interleave_on_scalar(256, 512)
        interleave(0, 256)
        gather(1, 512, 768)
        quantize_slots(0, 256)
        products((0, 1))
        for h in range(HALVES):
            for e in (0, 1):
                empty(e, h)
        interleave(512, 768)
        quantize_slots(256, 512)
        products((2, 3))
        empty(2, 0)
        empty(3, 0)
        quantize_slots(512, 768)
        products((4, 5))
        empty(4, 0)
        empty(5, 0)
        for e in range(2, E):
            empty(e, 1)
        quantize_tokens(256, 384)
        quantize_tokens(0, 256)
        shared(256, 384)
        shared(0, 256)

        def fetch(dst, h, g, lo, hi):
            nc.vector.tensor_tensor(
                dst[:, lo:hi],
                y[h][:].indirect((pos1_sb, pos2_sb)[g][:, lo // 16 : hi // 16]),
                gates[:, g, h, lo:hi],
                MULT,
            )

        def add_shared(h):
            nc.vector.scalar_tensor_tensor(partial[h][:], ys_ps[h][:], bias[:, h, E : E + 1], first[h][:], ADD, ADD)

        def finish(h, lo, hi):
            nc.vector.tensor_tensor(result[h][:, lo:hi], partial[h][:, lo:hi], second[h][:, lo:hi], ADD)
            nc.sync.dma_start(out=out[h * P : (h + 1) * P, lo:hi], in_=result[h][:, lo:hi])

        fetch(first[0], 0, 0, 0, T)
        fetch(second[0], 0, 1, 0, T)
        add_shared(0)
        fetch(first[1], 1, 0, 0, T)
        finish(0, 0, T)
        fetch(second[1], 1, 1, 0, 256)
        add_shared(1)
        fetch(second[1], 1, 1, 256, T)
        finish(1, 0, 256)
        finish(1, 256, T)
